import numpy as np
import ml_dtypes


def mxq(x, axis, fmt="e4m3"):
    dtype, down = {"e4m3": (ml_dtypes.float8_e4m3fn, 7), "e5m2": (ml_dtypes.float8_e5m2, 14)}[fmt]
    v = np.moveaxis(np.asarray(x, np.float32).astype(ml_dtypes.bfloat16).astype(np.float64), axis, -1)
    blocks = v.reshape(v.shape[:-1] + (-1, 32))
    amax = np.abs(blocks).max(-1, keepdims=True)
    byte = np.maximum(np.where(amax > 0, np.frexp(amax)[1] - 1 + 127, 0) - down, 1)
    scale = np.exp2(byte - 127.0)
    codes = (blocks / scale).astype(np.float32).astype(dtype).astype(np.float64)
    return np.moveaxis((codes * scale).reshape(v.shape), -1, axis)


WIDE = False


def mx_kscale(k):
    if not WIDE:
        return np.ones(k)
    levels = np.array([10, -10, 5, -5, 0])
    if k % 512:
        return np.exp2(np.random.permutation(np.resize(levels, k // 32))).repeat(32)
    a = np.empty((k // 512, 16))
    for p in range(k // 512):
        a[p, :8] = np.random.permutation(np.resize(levels, 8))
        for g in range(8):
            far = levels[np.abs(levels - a[p, g]) >= 10]
            a[p, g + 8] = far[np.random.randint(len(far))]
    return np.exp2(a.ravel()).repeat(32)


BF16 = ml_dtypes.bfloat16


def bf(x):
    return np.asarray(x, np.float32).astype(BF16)


def f64(x):
    return np.asarray(x).astype(np.float64)


E2M1 = np.array([0.0, 0.5, 1.0, 1.5, 2.0, 3.0, 4.0, 6.0, -0.0, -0.5, -1.0, -1.5, -2.0, -3.0, -4.0, -6.0])


def pack_weight(w, fmt):
    k, n = w.shape
    w = f64(bf(w)).reshape(k // 32, 32, n)
    amax = np.abs(w).max(1)
    if fmt == "e4m3":
        byte = np.frexp(amax)[1] - 1 + 127 - 7
    else:
        mant, ex = np.frexp(amax / 6.0)
        byte = np.where(mant > 0.5, ex, ex - 1) + 127
    byte = np.clip(np.where(amax > 0, byte, 1), 1, 254)
    scaled = (w * np.exp2(127.0 - byte)[:, None, :]).reshape(k, n).astype(np.float32)
    by_word = np.ascontiguousarray(scaled.reshape(k // 512, 128, 4, n).transpose(0, 1, 3, 2))
    if fmt == "e4m3":
        words = by_word.astype(ml_dtypes.float8_e4m3fn).view(np.uint8)
    else:
        c = by_word.astype(ml_dtypes.float4_e2m1fn).view(np.uint8) & 0xF
        words = c[..., 0::2] | (c[..., 1::2] << 4)
    return np.ascontiguousarray(words), np.ascontiguousarray(byte.astype(np.uint8).reshape(k // 512, 16, n))


def unpack_weight(words, scales, fmt):
    g, p, n, _ = words.shape
    if fmt == "e4m3":
        vals = np.ascontiguousarray(words).view(ml_dtypes.float8_e4m3fn).astype(np.float64)
    else:
        nib = np.empty((g, p, n, 4), np.uint8)
        nib[..., 0::2] = words & 0xF
        nib[..., 1::2] = words >> 4
        vals = E2M1[nib]
    vals = vals * np.repeat(np.exp2(scales.astype(np.float64) - 127.0), 8, axis=1)[..., None]
    return vals.transpose(0, 1, 3, 2).reshape(g * 512, n)
def pack4(w):
    words, scales = pack_weight(w, "e2m1")
    return words.reshape(words.shape[0], 128, -1), scales


def unpack4(words, scales):
    return unpack_weight(words.reshape(words.shape[0], 128, -1, 2), scales, "e2m1")


def planes(Y):
    n, m = Y.shape
    b = f64(bf(Y)).reshape(n // 32, 32, m)
    amax = np.abs(b).max(1)
    byte = np.clip(np.where(amax > 0, np.frexp(amax)[1] - 1 + 127 - 7, 1), 1, 254)
    codes = (b * np.exp2(127.0 - byte)[:, None, :]).reshape(n, m).astype(np.float32).astype(ml_dtypes.float8_e4m3fn).view(np.uint8)
    words = codes.reshape(n // 512, 128, 4, m).transpose(0, 1, 3, 2)
    return np.ascontiguousarray(words), np.ascontiguousarray(byte.astype(np.uint8).reshape(n // 512, 16, m))


M, K, R, V = 1024, 1536, 512, 2048

DRAFT_STD = 0.7
FULL_STD = 0.7


def setup_inputs():
    s = mx_kscale(R)
    r = mx_kscale(K)
    draft_state = np.random.randn(M, R) * s[None, :]
    draft_head = DRAFT_STD * np.random.randn(R, V) / np.sqrt(R) / s[:, None]
    full_state = np.random.randn(M, K) * r[None, :]
    full_head = FULL_STD * np.random.randn(K, V) / np.sqrt(K) / r[:, None]
    full_words, full_scales = pack4(full_head)
    bias = 0.3 * np.random.randn(V)
    cap = np.exp(0.8 * np.random.randn(V))
    return {"draft_state": bf(draft_state), "draft_head": bf(draft_head),
            "full_state": bf(full_state), "full_words": full_words, "full_scales": full_scales,
            "bias": bf(bias), "cap": bf(cap)}


def reference(draft_state, draft_head, full_state, full_words, full_scales, bias, cap):
    draft = mxq(f64(draft_state), 1, "e4m3") @ mxq(f64(draft_head), 0, "e4m3")
    correction = mxq(f64(full_state), 1, "e4m3") @ unpack4(full_words, full_scales)
    y = f64(cap) * np.tanh(draft + correction + f64(bias))
    Y = y.reshape(M, V).T
    words, scales = planes(Y)
    return y, words, scales

@@ -1,0 +1,354 @@
+from contextlib import ExitStack
+
+import concourse.mybir as mybir
+from concourse.masks import make_identity
+
+M, K, R, V = 1024, 1536, 512, 2048
+FLOPS = 2 * M * (K + R) * V
+
+F32 = mybir.dt.float32
+BF16 = mybir.dt.bfloat16
+I32 = mybir.dt.int32
+U32 = mybir.dt.uint32
+U8 = mybir.dt.uint8
+FP8X4 = mybir.dt.float8_e4m3fn_x4
+FP4X4 = mybir.dt.float4_e2m1fn_x4
+ADD = mybir.AluOpType.add
+MULT = mybir.AluOpType.mult
+TANH = mybir.ActivationFunctionType.Tanh
+
+P = 128
+PACK = 4
+GROUP = P * PACK
+FULL_PASSES = K // GROUP
+PASSES = FULL_PASSES + R // GROUP
+ROW_TILES = M // P
+GROUPS = V // GROUP
+CELLS = ROW_TILES * GROUPS
+PLANE_RUNS = [2] * 8 + [4, 4, 4, 2, 1, 1]
+HALF = CELLS // 2
+LATE_AT = 4
+TAIL_FROM = 24
+TAIL_LAG = 5
+VEC_HEAD = 0
+TURN_LAG = 5
+CAP_LAG = 2
+ROUND_LAG = 3
+VEC_EVERY = 4
+VEC_TAIL = 3
+HEAD_AT = 4
+Q_LAG = 2
+SPREAD = 1
+TANH_LAG = 1
+
+
+def tile_draft_full_logits_g5_kernel(
+    tc, draft_state, draft_head, full_state, full_words, full_scales, bias, cap, out_0, out_1, out_2
+):
+    nc = tc.nc
+
+    with ExitStack() as ctx:
+        keep = ctx.enter_context(tc.tile_pool(name="keep", bufs=1))
+        stage = ctx.enter_context(tc.tile_pool(name="stage", bufs=3))
+        psum = ctx.enter_context(tc.psum_pool(name="psum", bufs=8))
+        ctx.enter_context(tc.manual_schedule())
+
+        ident = keep.tile([P, P], F32, name="ident")
+        make_identity(nc, ident[:])
+
+        f_scales_first = keep.tile([P, FULL_PASSES, 2 * GROUP], U8, name="f_scales_first", align_bytes=64)
+        f_scales_rest = keep.tile([P, FULL_PASSES, 2 * GROUP], U8, name="f_scales_rest", align_bytes=64)
+        for plane in (f_scales_first, f_scales_rest):
+            nc.vector.memset(plane[:].rearrange("p c n -> p (c n)").bitcast(I32), 0)
+        bias_rows = keep.tile([P, V], BF16, name="bias_rows")
+        cap_rows = keep.tile([P, V], BF16, name="cap_rows")
+        y_scales = keep.tile([P, M], U8, name="y_scales", align_bytes=64)
+
+        full_raw, draft_raw, x_grouped, x_codes, x_scales = {}, {}, {}, {}, {}
+        f_words, h_raw, h_grouped, h_codes, h_scales, y_words = {}, {}, {}, {}, {}, {}
+        x_banks, acc, logits, squashed, y_f32, y_bf16, y_bank, y_grouped = {}, {}, {}, {}, {}, {}, {}, {}
+
+        place = [(cell % 2, cell // 2) if cell < HALF else divmod(cell, ROW_TILES) for cell in range(CELLS)]
+
+        def cols(g):
+            return slice(g * GROUP, (g + 1) * GROUP)
+
+        def load_full(m):
+            full_raw[m] = keep.tile([P, K], BF16, name="full_raw%d" % m)
+            nc.sync.dma_start(out=full_raw[m][:], in_=full_state[m * P : (m + 1) * P, :])
+
+        def load_draft(m):
+            draft_raw[m] = keep.tile([P, R], BF16, name="draft_raw%d" % m)
+            nc.sync.dma_start(out=draft_raw[m][:], in_=draft_state[m * P : (m + 1) * P, :])
+
+        def load_head(g):
+            h_raw[g] = keep.tile([P, PACK, GROUP], BF16, name="h_raw%d" % g)
+            nc.sync.dma_start(out=h_raw[g][:], in_=draft_head[:, cols(g)].rearrange("(p t) v -> p t v", t=PACK))
+
+        def load_words(g):
+            f_words[g] = keep.tile([P, FULL_PASSES, 2 * GROUP], U8, name="f_words%d" % g, align_bytes=64)
+            src = full_words.rearrange("c p n -> p c n")[:, :, 2 * g * GROUP : 2 * (g + 1) * GROUP]
+            nc.sync.dma_start(out=f_words[g][:].bitcast(I32), in_=src.bitcast(I32))
+
+        def load_scales(plane, span):
+            rows = full_scales.rearrange("c q n -> q c n")[:, :, span]
+            for quad in range(4):
+                nc.sync.dma_start(
+                    out=plane[32 * quad : 32 * quad + 4, :, :].bitcast(I32),
+                    in_=rows[4 * quad : 4 * quad + 4, :, :].bitcast(I32),
+                )
+
+        def load_row(rows, vector, span):
+            nc.sync.dma_start(out=rows[:, span], in_=vector[span].partition_broadcast(P))
+
+        def turn_x(m, half):
+            bank = psum.tile([P, 2, 2, P], F32, name="bank", tag="bank")
+            for c2 in range(2):
+                c = 2 * half + c2
+                if c < FULL_PASSES:
+                    words = full_raw[m][:].bitcast(F32)[:, c * 2 * P : (c + 1) * 2 * P]
+                else:
+                    words = draft_raw[m][:].bitcast(F32)
+                for u in range(2):
+                    nc.tensor.transpose(bank[:, c2, u, :], words[:, u::2], ident[:])
+            x_banks[m, half] = bank
+
+        def copy_x(m, half):
+            if half == 0:
+                x_grouped[m] = stage.tile([P, PASSES * GROUP], BF16, name="x_grouped", align_bytes=64)
+            words = x_grouped[m][:, half * 2 * GROUP : (half + 1) * 2 * GROUP].bitcast(F32)
+            nc.scalar.copy(
+                out=words.rearrange("p (c r u) -> p c r u", c=2, u=2),
+                in_=x_banks[m, half][:].rearrange("p c u r -> p c r u"),
+            )
+
+        def quantize_x(m, first_pass, passes):
+            if first_pass == 0:
+                x_codes[m] = keep.tile([P, PASSES * P], U32, name="x_codes%d" % m, align_bytes=64)
+                x_scales[m] = keep.tile([P, PASSES * P], U8, name="x_scales%d" % m, align_bytes=64)
+            span = slice(first_pass * P, (first_pass + passes) * P)
+            nc.vector.quantize_mx(
+                out=x_codes[m][:, span].bitcast(FP8X4),
+                scales=x_scales[m][:, span],
+                in_=x_grouped[m][:, first_pass * GROUP : (first_pass + passes) * GROUP],
+            )
+
+        def group_head(g, part, parts, on_scalar):
+            if part == 0:
+                h_grouped[g] = stage.tile([P, GROUP, PACK], BF16, name="h_grouped", align_bytes=64, bufs=2)
+            span = slice(part * GROUP // parts, (part + 1) * GROUP // parts)
+            dst = h_grouped[g][:, span, :].rearrange("p (a i) t -> p a t i", i=4)
+            src = h_raw[g][:, :, span].rearrange("p t (a i) -> p a t i", i=4)
+            if on_scalar:
+                nc.scalar.copy(out=dst, in_=src)
+            else:
+                nc.vector.tensor_copy(out=dst, in_=src)
+
+        def quantize_head(g):
+            h_codes[g] = keep.tile([P, GROUP], U32, name="h_codes%d" % g, align_bytes=64)
+            h_scales[g] = keep.tile([P, GROUP], U8, name="h_scales%d" % g, align_bytes=64)
+            nc.vector.quantize_mx(
+                out=h_codes[g][:].bitcast(FP8X4),
+                scales=h_scales[g][:],
+                in_=h_grouped[g][:].rearrange("p v t -> p (v t)"),
+            )
+
+        def multiply(cell):
+            g, m = place[cell]
+            acc[cell] = psum.tile([P, GROUP], F32, name="bank", tag="bank")
+            for c in range(PASSES):
+                if c < FULL_PASSES:
+                    rhs = f_words[g][:, c, :].bitcast(FP4X4)
+                    rhs_scale = (f_scales_first if g < 2 else f_scales_rest)[:, c, cols(g % 2)]
+                else:
+                    rhs, rhs_scale = h_codes[g][:].bitcast(FP8X4), h_scales[g][:]
+                nc.tensor.matmul_mx(
+                    out=acc[cell][:],
+                    lhsT=x_codes[m][:, c * P : (c + 1) * P].bitcast(FP8X4),
+                    lhsT_scale=x_scales[m][:, c * P : (c + 1) * P],
+                    rhs=rhs,
+                    rhs_scale=rhs_scale,
+                    start=(c == 0),
+                    stop=(c == PASSES - 1),
+                )
+
+        def runs_of(sizes):
+            owner, first = {}, 0
+            for size in sizes:
+                for cell in range(first, first + size):
+                    owner[cell] = (first, size)
+                first += size
+            return owner
+
+        stores = runs_of([2] * (CELLS // 2 - 1) + [1, 1])
+        turns = runs_of(PLANE_RUNS)
+
+        def add_bias(cell):
+            logits[cell] = stage.tile([P, GROUP], F32, name="logits", bufs=4)
+            nc.vector.tensor_tensor(out=logits[cell][:], in0=acc[cell][:], in1=bias_rows[:, cols(place[cell][0])], op=ADD)
+
+        def squash(cell):
+            squashed[cell] = stage.tile([P, GROUP], F32, name="squashed", bufs=4)
+            nc.scalar.activation(out=squashed[cell][:], in_=logits[cell][:], func=TANH)
+
+        def scale_and_store(cell):
+            first, count = stores[cell]
+            g, m = place[cell]
+            if cell == first:
+                y_f32[first] = stage.tile([P, count, GROUP], F32, name="y_f32", bufs=5)
+            nc.vector.tensor_tensor(
+                out=y_f32[first][:, cell - first, :], in0=squashed[cell][:], in1=cap_rows[:, cols(g)], op=MULT
+            )
+            if cell == first + count - 1:
+                g0, m0 = place[first]
+                block = out_0[m0 * P : (m + 1) * P, g0 * GROUP : (g + 1) * GROUP]
+                pattern = "(j p) v -> p j v" if g0 == g else "p (j v) -> p j v"
+                nc.sync.dma_start(out=block.rearrange(pattern, j=count), in_=y_f32[first][:])
+
+        def round_y(cell, on_scalar):
+            y_bf16[cell] = stage.tile([P, 2, P, 2], BF16, name="y_bf16", bufs=8)
+            first = stores[cell][0]
+            src = y_f32[first][:, cell - first, :].rearrange("p (q u e) -> p u q e", u=2, e=2)
+            if on_scalar:
+                nc.scalar.copy(out=y_bf16[cell][:], in_=src)
+            else:
+                nc.vector.tensor_copy(out=y_bf16[cell][:], in_=src)
+
+        def turn_y(first, count):
+            for pair in range(first, first + count, 2):
+                width = min(2, count)
+                y_bank[pair] = psum.tile([P, width, 2, P], F32, name="bank", tag="bank")
+                for j in range(width):
+                    words = y_bf16[pair + j][:].rearrange("p u q e -> p (u q e)").bitcast(F32)
+                    for u in range(2):
+                        nc.tensor.transpose(y_bank[pair][:, j, u, :], words[:, u * P : (u + 1) * P], ident[:])
+
+        def copy_y(pair, width):
+            y_grouped[pair] = stage.tile([P, width * GROUP], BF16, name="y_grouped", align_bytes=64, bufs=4)
+            nc.scalar.copy(
+                out=y_grouped[pair][:].bitcast(F32).rearrange("p (j r u) -> p j r u", j=width, u=2),
+                in_=y_bank[pair][:].rearrange("p j u r -> p j r u"),
+            )
+
+        def store_words(g, span):
+            dst = out_1[g].rearrange("p m t -> p (m t)").bitcast(I32)
+            nc.sync.dma_start(out=dst[:, span], in_=y_words[g][:, span].bitcast(I32))
+
+        def quantize_y(pair, at, width):
+            g, m = place[pair + at]
+            if m == 0:
+                y_words[g] = keep.tile([P, M], U32, name="y_words%d" % g, align_bytes=64)
+            nc.vector.quantize_mx(
+                out=y_words[g][:, m * P : (m + width) * P].bitcast(FP8X4),
+                scales=y_scales[4 * g :, m * P : (m + width) * P],
+                in_=y_grouped[pair][:, at * GROUP : (at + width) * GROUP],
+            )
+            done = (m + width) * P
+            if g < GROUPS - 1:
+                if done == M:
+                    store_words(g, slice(0, M))
+            elif done == M - 2 * P:
+                store_words(g, slice(0, done))
+            elif done == M:
+                store_words(g, slice(M - 2 * P, M))
+                for quad in range(4):
+                    queue = nc.sync if quad < 2 else nc.scalar
+                    queue.dma_start(
+                        out=out_2[:, 4 * quad : 4 * quad + 4, :].bitcast(I32),
+                        in_=y_scales[32 * quad : 32 * quad + 16, :].bitcast(I32),
+                    )
+
+        turn_at, copy_at, quant_at = {}, {}, {}
+        for first, count in sorted(set(turns.values())):
+            when = first + count - 1 + (TURN_LAG if first < TAIL_FROM else TAIL_LAG)
+            turn_at[when] = (first, count)
+            for pair in range(first, first + count, 2):
+                width = min(2, count)
+                copied = when + (pair - first) // 2 * SPREAD
+                copy_at.setdefault(copied, []).append((pair, width))
+                if pair < HALF:
+                    for at in range(2):
+                        quant_at.setdefault(copied + Q_LAG + at, []).append((pair, at, 1))
+                else:
+                    quant_at.setdefault(copied + Q_LAG, []).append((pair, 0, width))
+
+        load_full(0)
+        load_head(0)
+        load_draft(0)
+        load_words(0)
+        load_scales(f_scales_first, slice(0, 2 * GROUP))
+        load_head(1)
+        load_full(1)
+        load_draft(1)
+        load_row(bias_rows, bias, cols(0))
+        load_words(1)
+        load_row(cap_rows, cap, cols(0))
+        load_full(2)
+        load_draft(2)
+        load_row(bias_rows, bias, cols(1))
+        load_row(cap_rows, cap, cols(1))
+        for m in range(3, ROW_TILES):
+            load_full(m)
+            load_draft(m)
+            if m in (3, 4):
+                load_head(m - 1)
+
+        for half in range(2):
+            turn_x(0, half)
+            copy_x(0, half)
+        group_head(0, 0, 1, False)
+        quantize_x(0, 0, 2)
+        quantize_head(0)
+        quantize_x(0, 2, 2)
+        group_head(1, 0, 1, False)
+
+        for step in range(max(quant_at) + 1):
+            if step == LATE_AT:
+                load_words(2)
+                load_scales(f_scales_rest, slice(2 * GROUP, V))
+                load_row(bias_rows, bias, slice(2 * GROUP, V))
+                load_row(cap_rows, cap, slice(2 * GROUP, V))
+            if step == LATE_AT + 4:
+                load_words(3)
+            ahead = []
+            if step == 1:
+                ahead = [1]
+            elif step >= 2 and step % 2 == 0 and step // 2 + 1 < ROW_TILES:
+                ahead = [step // 2 + 1]
+            if step == 2:
+                quantize_x(1, 0, PASSES)
+            for m in ahead:
+                for half in range(2):
+                    turn_x(m, half)
+            if step in turn_at:
+                turn_y(*turn_at[step])
+            if step == 1:
+                quantize_head(1)
+            if step < CELLS:
+                multiply(step)
+            if 0 <= step - 1 < CELLS:
+                add_bias(step - 1)
+            if step == 1:
+                squash(0)
+            for m in ahead:
+                for half in range(2):
+                    copy_x(m, half)
+            if 1 <= step - TANH_LAG < CELLS:
+                squash(step - TANH_LAG)
+            if 0 <= step - CAP_LAG < CELLS:
+                scale_and_store(step - CAP_LAG)
+            if step >= 3 and step % 2 == 1 and step // 2 + 1 < ROW_TILES:
+                quantize_x(step // 2 + 1, 0, PASSES)
+            for job in quant_at.get(step, []):
+                quantize_y(*job)
+            cell = step - ROUND_LAG
+            if 0 <= cell < CELLS:
+                round_y(cell, cell % VEC_EVERY != VEC_EVERY - 1 and VEC_HEAD <= cell < CELLS - VEC_TAIL)
+            for job in copy_at.get(step, []):
+                copy_y(*job)
+            g, part = divmod(step - HEAD_AT, 4)
+            if 0 <= g < 2:
+                if part in (0, 2):
+                    group_head(g + 2, part // 2, 2, False)
+                if part == 3:
+                    quantize_head(g + 2)

@@ -28,18 +28,20 @@ CELLS = ROW_TILES * GROUPS
 PLANE_RUNS = [2] * 8 + [4, 4, 4, 2, 1, 1]
 HALF = CELLS // 2
 LATE_AT = 4
-TAIL_FROM = 24
-TAIL_LAG = 5
+POOL = False
+HS = False
+TAIL_FROM = 28
+TAIL_LAG = 6
 VEC_HEAD = 0
-TURN_LAG = 5
-CAP_LAG = 2
-ROUND_LAG = 3
-VEC_EVERY = 4
+TURN_LAG = 7
+CAP_LAG = 3
+ROUND_LAG = 4
+VEC_EVERY = 8
 VEC_TAIL = 3
-HEAD_AT = 4
+HEAD_AT = 2
 Q_LAG = 2
 SPREAD = 1
-TANH_LAG = 1
+TANH_LAG = 2
 
 
 def tile_draft_full_logits_g5_kernel(
@@ -98,8 +100,21 @@ def tile_draft_full_logits_g5_kernel(
                     in_=rows[4 * quad : 4 * quad + 4, :, :].bitcast(I32),
                 )
 
-        def load_row(rows, vector, span):
-            nc.sync.dma_start(out=rows[:, span], in_=vector[span].partition_broadcast(P))
+        def load_vector(vector, name):
+            lines = keep.tile([P, 2, 2 * PACK], BF16, name=name)
+            nc.sync.dma_start(out=lines[:], in_=vector.rearrange("(h n e) -> n h e", h=2, n=P))
+            return lines
+
+        def spread_turn(lines, h):
+            bank = psum.tile([P, PACK, P], F32, name="bank", tag="bank")
+            words = lines[:, h, :].bitcast(F32)
+            for i in range(PACK):
+                nc.tensor.transpose(bank[:, i, :], words[:, i : i + 1].to_broadcast([P, P]), ident[:])
+            return bank
+
+        def spread_copy(bank, rows, h):
+            words = rows[:, h * 2 * GROUP : (h + 1) * 2 * GROUP].bitcast(F32)
+            nc.scalar.copy(out=words.rearrange("p (n i) -> p n i", i=PACK), in_=bank[:].rearrange("p i n -> p n i"))
 
         def turn_x(m, half):
             bank = psum.tile([P, 2, 2, P], F32, name="bank", tag="bank")
@@ -209,7 +224,9 @@ def tile_draft_full_logits_g5_kernel(
             y_bf16[cell] = stage.tile([P, 2, P, 2], BF16, name="y_bf16", bufs=8)
             first = stores[cell][0]
             src = y_f32[first][:, cell - first, :].rearrange("p (q u e) -> p u q e", u=2, e=2)
-            if on_scalar:
+            if on_scalar and POOL:
+                nc.gpsimd.tensor_scalar(out=y_bf16[cell][:], in0=src, scalar1=1.0, scalar2=0.0, op0=MULT, op1=ADD)
+            elif on_scalar:
                 nc.scalar.copy(out=y_bf16[cell][:], in_=src)
             else:
                 nc.vector.tensor_copy(out=y_bf16[cell][:], in_=src)
@@ -243,14 +260,11 @@ def tile_draft_full_logits_g5_kernel(
                 scales=y_scales[4 * g :, m * P : (m + width) * P],
                 in_=y_grouped[pair][:, at * GROUP : (at + width) * GROUP],
             )
+            marks = [0, M // 2, M] if g < GROUPS - 1 else [0, M // 2, M - 2 * P, M]
             done = (m + width) * P
-            if g < GROUPS - 1:
-                if done == M:
-                    store_words(g, slice(0, M))
-            elif done == M - 2 * P:
-                store_words(g, slice(0, done))
-            elif done == M:
-                store_words(g, slice(M - 2 * P, M))
+            if done in marks:
+                store_words(g, slice(marks[marks.index(done) - 1], done))
+            if g == GROUPS - 1 and done == M:
                 for quad in range(4):
                     queue = nc.sync if quad < 2 else nc.scalar
                     queue.dma_start(
@@ -272,7 +286,9 @@ def tile_draft_full_logits_g5_kernel(
                 else:
                     quant_at.setdefault(copied + Q_LAG, []).append((pair, 0, width))
 
+        bias_lines = load_vector(bias, "bias_lines")
         load_full(0)
+        cap_lines = load_vector(cap, "cap_lines")
         load_head(0)
         load_draft(0)
         load_words(0)
@@ -280,22 +296,20 @@ def tile_draft_full_logits_g5_kernel(
         load_head(1)
         load_full(1)
         load_draft(1)
-        load_row(bias_rows, bias, cols(0))
         load_words(1)
-        load_row(cap_rows, cap, cols(0))
         load_full(2)
         load_draft(2)
-        load_row(bias_rows, bias, cols(1))
-        load_row(cap_rows, cap, cols(1))
         for m in range(3, ROW_TILES):
             load_full(m)
             load_draft(m)
             if m in (3, 4):
                 load_head(m - 1)
 
+        spread_copy(spread_turn(bias_lines, 0), bias_rows, 0)
         for half in range(2):
             turn_x(0, half)
             copy_x(0, half)
+        spread_copy(spread_turn(cap_lines, 0), cap_rows, 0)
         group_head(0, 0, 1, False)
         quantize_x(0, 0, 2)
         quantize_head(0)
@@ -306,8 +320,6 @@ def tile_draft_full_logits_g5_kernel(
             if step == LATE_AT:
                 load_words(2)
                 load_scales(f_scales_rest, slice(2 * GROUP, V))
-                load_row(bias_rows, bias, slice(2 * GROUP, V))
-                load_row(cap_rows, cap, slice(2 * GROUP, V))
             if step == LATE_AT + 4:
                 load_words(3)
             ahead = []
@@ -317,6 +329,10 @@ def tile_draft_full_logits_g5_kernel(
                 ahead = [step // 2 + 1]
             if step == 2:
                 quantize_x(1, 0, PASSES)
+            if step == HALF - 2:
+                spread_copy(spread_turn(bias_lines, 1), bias_rows, 1)
+            if step == HALF:
+                spread_copy(spread_turn(cap_lines, 1), cap_rows, 1)
             for m in ahead:
                 for half in range(2):
                     turn_x(m, half)
@@ -349,6 +365,6 @@ def tile_draft_full_logits_g5_kernel(
             g, part = divmod(step - HEAD_AT, 4)
             if 0 <= g < 2:
                 if part in (0, 2):
-                    group_head(g + 2, part // 2, 2, False)
+                    group_head(g + 2, part // 2, 2, HS)
                 if part == 3:
                     quantize_head(g + 2)

@@ -20,28 +20,20 @@ TANH = mybir.ActivationFunctionType.Tanh
 P = 128
 PACK = 4
 GROUP = P * PACK
+WIDE = 2 * GROUP
 FULL_PASSES = K // GROUP
 PASSES = FULL_PASSES + R // GROUP
 ROW_TILES = M // P
-GROUPS = V // GROUP
-CELLS = ROW_TILES * GROUPS
-PLANE_RUNS = [2] * 8 + [4, 4, 4, 2, 1, 1]
-HALF = CELLS // 2
-LATE_AT = 4
-POOL = False
-HS = False
-TAIL_FROM = 28
-TAIL_LAG = 6
-VEC_HEAD = 0
-TURN_LAG = 7
-CAP_LAG = 3
-ROUND_LAG = 4
-VEC_EVERY = 8
-VEC_TAIL = 3
-HEAD_AT = 2
-Q_LAG = 2
-SPREAD = 1
-TANH_LAG = 2
+CELLS = ROW_TILES * V // GROUP
+STEPS = CELLS // 4
+BANKS = 8
+QUADRANTS = 4
+MX_ALIGN = 64
+
+PRELOADED = 5
+SORTED_FROM = 3
+TURN_LAG = 4
+WORD_MARKS = [0, M // 2, M - 2 * P, M]
 
 
 def tile_draft_full_logits_g5_kernel(
@@ -52,51 +44,64 @@ def tile_draft_full_logits_g5_kernel(
     with ExitStack() as ctx:
         keep = ctx.enter_context(tc.tile_pool(name="keep", bufs=1))
         stage = ctx.enter_context(tc.tile_pool(name="stage", bufs=3))
-        psum = ctx.enter_context(tc.psum_pool(name="psum", bufs=8))
+        psum = ctx.enter_context(tc.psum_pool(name="psum", bufs=1))
         ctx.enter_context(tc.manual_schedule())
 
         ident = keep.tile([P, P], F32, name="ident")
         make_identity(nc, ident[:])
 
-        f_scales_first = keep.tile([P, FULL_PASSES, 2 * GROUP], U8, name="f_scales_first", align_bytes=64)
-        f_scales_rest = keep.tile([P, FULL_PASSES, 2 * GROUP], U8, name="f_scales_rest", align_bytes=64)
-        for plane in (f_scales_first, f_scales_rest):
+        f_scales = []
+        for h in range(2):
+            plane = keep.tile([P, FULL_PASSES, WIDE], U8, name="f_scales%d" % h, align_bytes=MX_ALIGN)
             nc.vector.memset(plane[:].rearrange("p c n -> p (c n)").bitcast(I32), 0)
+            f_scales.append(plane)
         bias_rows = keep.tile([P, V], BF16, name="bias_rows")
-        cap_rows = keep.tile([P, V], BF16, name="cap_rows")
-        y_scales = keep.tile([P, M], U8, name="y_scales", align_bytes=64)
+        y_scales = keep.tile([P, M], U8, name="y_scales", align_bytes=MX_ALIGN)
 
-        full_raw, draft_raw, x_grouped, x_codes, x_scales = {}, {}, {}, {}, {}
-        f_words, h_raw, h_grouped, h_codes, h_scales, y_words = {}, {}, {}, {}, {}, {}
-        x_banks, acc, logits, squashed, y_f32, y_bf16, y_bank, y_grouped = {}, {}, {}, {}, {}, {}, {}, {}
+        x_raw, x_sorted, x_banks, x_grouped, x_codes, x_scales = {}, {}, {}, {}, {}, {}
+        f_words, h_raw, h_grouped, h_codes, h_scales = {}, {}, {}, {}, {}
+        cap_banks, acc, logits, squashed, y_f32 = {}, {}, {}, {}, {}
+        y_bf16, y_banks, y_grouped, y_words = {}, {}, {}, {}
 
-        place = [(cell % 2, cell // 2) if cell < HALF else divmod(cell, ROW_TILES) for cell in range(CELLS)]
+        pairs = [(0, 0), (0, 1), (1, 0), (1, 1)] + [(h, m) for m in range(2, ROW_TILES) for h in range(2)]
+        place = [(2 * h + side, m) for h, m in pairs for side in range(2)]
+
+        free_banks = list(range(BANKS))
+
+        def next_bank(shape, hold=False):
+            number = free_banks.pop(0)
+            if not hold:
+                free_banks.append(number)
+            return psum.tile(shape, F32, name="bank%d" % number)
 
         def cols(g):
             return slice(g * GROUP, (g + 1) * GROUP)
 
+        def wide(h):
+            return slice(h * WIDE, (h + 1) * WIDE)
+
+
         def load_full(m):
-            full_raw[m] = keep.tile([P, K], BF16, name="full_raw%d" % m)
-            nc.sync.dma_start(out=full_raw[m][:], in_=full_state[m * P : (m + 1) * P, :])
+            x_raw[m] = keep.tile([P, K + R], BF16, name="x_raw%d" % m)
+            nc.sync.dma_start(out=x_raw[m][:, :K], in_=full_state[m * P : (m + 1) * P, :])
 
         def load_draft(m):
-            draft_raw[m] = keep.tile([P, R], BF16, name="draft_raw%d" % m)
-            nc.sync.dma_start(out=draft_raw[m][:], in_=draft_state[m * P : (m + 1) * P, :])
+            nc.sync.dma_start(out=x_raw[m][:, K:], in_=draft_state[m * P : (m + 1) * P, :])
 
         def load_head(g):
             h_raw[g] = keep.tile([P, PACK, GROUP], BF16, name="h_raw%d" % g)
             nc.sync.dma_start(out=h_raw[g][:], in_=draft_head[:, cols(g)].rearrange("(p t) v -> p t v", t=PACK))
 
         def load_words(g):
-            f_words[g] = keep.tile([P, FULL_PASSES, 2 * GROUP], U8, name="f_words%d" % g, align_bytes=64)
+            f_words[g] = keep.tile([P, FULL_PASSES, 2 * GROUP], U8, name="f_words%d" % g, align_bytes=MX_ALIGN)
             src = full_words.rearrange("c p n -> p c n")[:, :, 2 * g * GROUP : 2 * (g + 1) * GROUP]
             nc.sync.dma_start(out=f_words[g][:].bitcast(I32), in_=src.bitcast(I32))
 
-        def load_scales(plane, span):
-            rows = full_scales.rearrange("c q n -> q c n")[:, :, span]
-            for quad in range(4):
+        def load_scales(h):
+            rows = full_scales.rearrange("c q n -> q c n")[:, :, wide(h)]
+            for quad in range(QUADRANTS):
                 nc.sync.dma_start(
-                    out=plane[32 * quad : 32 * quad + 4, :, :].bitcast(I32),
+                    out=f_scales[h][32 * quad : 32 * quad + 4, :, :].bitcast(I32),
                     in_=rows[4 * quad : 4 * quad + 4, :, :].bitcast(I32),
                 )
 
@@ -105,42 +110,52 @@ def tile_draft_full_logits_g5_kernel(
             nc.sync.dma_start(out=lines[:], in_=vector.rearrange("(h n e) -> n h e", h=2, n=P))
             return lines
 
-        def spread_turn(lines, h):
-            bank = psum.tile([P, PACK, P], F32, name="bank", tag="bank")
-            words = lines[:, h, :].bitcast(F32)
+
+        def spread_bias(h):
+            bank = next_bank([P, PACK, P])
+            words = bias_lines[:, h, :].bitcast(F32)
             for i in range(PACK):
                 nc.tensor.transpose(bank[:, i, :], words[:, i : i + 1].to_broadcast([P, P]), ident[:])
             return bank
 
-        def spread_copy(bank, rows, h):
-            words = rows[:, h * 2 * GROUP : (h + 1) * 2 * GROUP].bitcast(F32)
-            nc.scalar.copy(out=words.rearrange("p (n i) -> p n i", i=PACK), in_=bank[:].rearrange("p i n -> p n i"))
+        def copy_bias(bank, h):
+            words = bias_rows[:, wide(h)].bitcast(F32).rearrange("p (n i) -> p n i", i=PACK)
+            nc.scalar.copy(out=words, in_=bank[:].rearrange("p i n -> p n i"))
+
+        def spread_cap(h):
+            cap_banks[h] = next_bank([P, P, PACK], hold=True)
+            words = cap_lines[:, h, :].bitcast(F32)
+            for i in range(PACK):
+                nc.tensor.transpose(cap_banks[h][:, :, i], words[:, i : i + 1].to_broadcast([P, P]), ident[:])
+
+
+        def x_words(m, half):
+            words = x_raw[m][:, wide(half)].bitcast(F32)
+            return words.rearrange("p (c q u) -> p c u q", c=2, u=2)
+
+        def sort_x(m, half, copy):
+            x_sorted[m, half] = stage.tile([P, 2, 2, P], F32, name="x_sorted", bufs=6)
+            copy(out=x_sorted[m, half][:], in_=x_words(m, half))
 
         def turn_x(m, half):
-            bank = psum.tile([P, 2, 2, P], F32, name="bank", tag="bank")
-            for c2 in range(2):
-                c = 2 * half + c2
-                if c < FULL_PASSES:
-                    words = full_raw[m][:].bitcast(F32)[:, c * 2 * P : (c + 1) * 2 * P]
-                else:
-                    words = draft_raw[m][:].bitcast(F32)
+            x_banks[m, half] = next_bank([P, 2, 2, P])
+            source = x_sorted[m, half][:] if m >= SORTED_FROM else x_words(m, half)
+            for c in range(2):
                 for u in range(2):
-                    nc.tensor.transpose(bank[:, c2, u, :], words[:, u::2], ident[:])
-            x_banks[m, half] = bank
+                    nc.tensor.transpose(x_banks[m, half][:, c, u, :], source[:, c, u, :], ident[:])
 
         def copy_x(m, half):
             if half == 0:
-                x_grouped[m] = stage.tile([P, PASSES * GROUP], BF16, name="x_grouped", align_bytes=64)
-            words = x_grouped[m][:, half * 2 * GROUP : (half + 1) * 2 * GROUP].bitcast(F32)
+                x_grouped[m] = stage.tile([P, PASSES * GROUP], BF16, name="x_grouped", align_bytes=MX_ALIGN)
             nc.scalar.copy(
-                out=words.rearrange("p (c r u) -> p c r u", c=2, u=2),
+                out=x_grouped[m][:, wide(half)].bitcast(F32).rearrange("p (c r u) -> p c r u", c=2, u=2),
                 in_=x_banks[m, half][:].rearrange("p c u r -> p c r u"),
             )
 
         def quantize_x(m, first_pass, passes):
             if first_pass == 0:
-                x_codes[m] = keep.tile([P, PASSES * P], U32, name="x_codes%d" % m, align_bytes=64)
-                x_scales[m] = keep.tile([P, PASSES * P], U8, name="x_scales%d" % m, align_bytes=64)
+                x_codes[m] = keep.tile([P, PASSES * P], U32, name="x_codes%d" % m, align_bytes=MX_ALIGN)
+                x_scales[m] = keep.tile([P, PASSES * P], U8, name="x_scales%d" % m, align_bytes=MX_ALIGN)
             span = slice(first_pass * P, (first_pass + passes) * P)
             nc.vector.quantize_mx(
                 out=x_codes[m][:, span].bitcast(FP8X4),
@@ -148,33 +163,30 @@ def tile_draft_full_logits_g5_kernel(
                 in_=x_grouped[m][:, first_pass * GROUP : (first_pass + passes) * GROUP],
             )
 
-        def group_head(g, part, parts, on_scalar):
-            if part == 0:
-                h_grouped[g] = stage.tile([P, GROUP, PACK], BF16, name="h_grouped", align_bytes=64, bufs=2)
-            span = slice(part * GROUP // parts, (part + 1) * GROUP // parts)
-            dst = h_grouped[g][:, span, :].rearrange("p (a i) t -> p a t i", i=4)
-            src = h_raw[g][:, :, span].rearrange("p t (a i) -> p a t i", i=4)
-            if on_scalar:
-                nc.scalar.copy(out=dst, in_=src)
-            else:
-                nc.vector.tensor_copy(out=dst, in_=src)
+
+        def group_head(g):
+            h_grouped[g] = stage.tile([P, GROUP, PACK], BF16, name="h_grouped", align_bytes=MX_ALIGN, bufs=2)
+            nc.vector.tensor_copy(
+                out=h_grouped[g][:].rearrange("p (a i) t -> p a t i", i=4),
+                in_=h_raw[g][:].rearrange("p t (a i) -> p a t i", i=4),
+            )
 
         def quantize_head(g):
-            h_codes[g] = keep.tile([P, GROUP], U32, name="h_codes%d" % g, align_bytes=64)
-            h_scales[g] = keep.tile([P, GROUP], U8, name="h_scales%d" % g, align_bytes=64)
+            h_codes[g] = keep.tile([P, GROUP], U32, name="h_codes%d" % g, align_bytes=MX_ALIGN)
+            h_scales[g] = keep.tile([P, GROUP], U8, name="h_scales%d" % g, align_bytes=MX_ALIGN)
             nc.vector.quantize_mx(
                 out=h_codes[g][:].bitcast(FP8X4),
                 scales=h_scales[g][:],
                 in_=h_grouped[g][:].rearrange("p v t -> p (v t)"),
             )
 
+
         def multiply(cell):
             g, m = place[cell]
-            acc[cell] = psum.tile([P, GROUP], F32, name="bank", tag="bank")
+            acc[cell] = next_bank([P, GROUP])
             for c in range(PASSES):
                 if c < FULL_PASSES:
-                    rhs = f_words[g][:, c, :].bitcast(FP4X4)
-                    rhs_scale = (f_scales_first if g < 2 else f_scales_rest)[:, c, cols(g % 2)]
+                    rhs, rhs_scale = f_words[g][:, c, :].bitcast(FP4X4), f_scales[g // 2][:, c, cols(g % 2)]
                 else:
                     rhs, rhs_scale = h_codes[g][:].bitcast(FP8X4), h_scales[g][:]
                 nc.tensor.matmul_mx(
@@ -187,104 +199,87 @@ def tile_draft_full_logits_g5_kernel(
                     stop=(c == PASSES - 1),
                 )
 
-        def runs_of(sizes):
-            owner, first = {}, 0
-            for size in sizes:
-                for cell in range(first, first + size):
-                    owner[cell] = (first, size)
-                first += size
-            return owner
-
-        stores = runs_of([2] * (CELLS // 2 - 1) + [1, 1])
-        turns = runs_of(PLANE_RUNS)
-
         def add_bias(cell):
-            logits[cell] = stage.tile([P, GROUP], F32, name="logits", bufs=4)
-            nc.vector.tensor_tensor(out=logits[cell][:], in0=acc[cell][:], in1=bias_rows[:, cols(place[cell][0])], op=ADD)
+            pair, side = divmod(cell, 2)
+            if side == 0:
+                logits[pair] = stage.tile([P, WIDE], F32, name="logits")
+            nc.vector.tensor_tensor(
+                out=logits[pair][:, cols(side)], in0=acc[cell][:], in1=bias_rows[:, cols(place[cell][0])], op=ADD
+            )
 
         def squash(cell):
-            squashed[cell] = stage.tile([P, GROUP], F32, name="squashed", bufs=4)
-            nc.scalar.activation(out=squashed[cell][:], in_=logits[cell][:], func=TANH)
+            pair, side = divmod(cell, 2)
+            if side == 0:
+                squashed[pair] = stage.tile([P, WIDE], F32, name="squashed")
+            nc.scalar.activation(out=squashed[pair][:, cols(side)], in_=logits[pair][:, cols(side)], func=TANH)
 
-        def scale_and_store(cell):
-            first, count = stores[cell]
-            g, m = place[cell]
-            if cell == first:
-                y_f32[first] = stage.tile([P, count, GROUP], F32, name="y_f32", bufs=5)
-            nc.vector.tensor_tensor(
-                out=y_f32[first][:, cell - first, :], in0=squashed[cell][:], in1=cap_rows[:, cols(g)], op=MULT
+        def scale_and_store(cell, count):
+            pair, side = divmod(cell, 2)
+            h, m = pairs[pair]
+            if side == 0:
+                y_f32[pair] = stage.tile([P, WIDE], F32, name="y_f32", bufs=5)
+            span = slice(side * GROUP, (side + count) * GROUP)
+            caps = cap_banks[h][:].rearrange("p n i -> p (n i)").bitcast(BF16)
+            nc.vector.tensor_tensor(out=y_f32[pair][:, span], in0=squashed[pair][:, span], in1=caps[:, span], op=MULT)
+            nc.sync.dma_start(out=out_0[m * P : (m + 1) * P, wide(h)][:, span], in_=y_f32[pair][:, span])
+
+
+        def round_on_gpsimd(out, in_):
+            nc.gpsimd.tensor_scalar(out=out, in0=in_, scalar1=1.0, scalar2=-0.0, op0=MULT, op1=ADD)
+
+        def round_y(cell, convert):
+            y_bf16[cell] = stage.tile([P, 2, P, 2], BF16, name="y_bf16", bufs=14)
+            src = y_f32[cell // 2][:, cols(cell % 2)].rearrange("p (q u e) -> p u q e", u=2, e=2)
+            convert(out=y_bf16[cell][:], in_=src)
+
+        def turn_y(cells):
+            y_banks[cells] = next_bank([P, len(cells), 2, P])
+            for j, cell in enumerate(cells):
+                words = y_bf16[cell][:].rearrange("p u q e -> p u (q e)").bitcast(F32)
+                for u in range(2):
+                    nc.tensor.transpose(y_banks[cells][:, j, u, :], words[:, u, :], ident[:])
+
+        def copy_y(cells):
+            y_grouped[cells] = stage.tile(
+                [P, len(cells) * GROUP], BF16, name="y_grouped", align_bytes=MX_ALIGN, bufs=6
             )
-            if cell == first + count - 1:
-                g0, m0 = place[first]
-                block = out_0[m0 * P : (m + 1) * P, g0 * GROUP : (g + 1) * GROUP]
-                pattern = "(j p) v -> p j v" if g0 == g else "p (j v) -> p j v"
-                nc.sync.dma_start(out=block.rearrange(pattern, j=count), in_=y_f32[first][:])
-
-        def round_y(cell, on_scalar):
-            y_bf16[cell] = stage.tile([P, 2, P, 2], BF16, name="y_bf16", bufs=8)
-            first = stores[cell][0]
-            src = y_f32[first][:, cell - first, :].rearrange("p (q u e) -> p u q e", u=2, e=2)
-            if on_scalar and POOL:
-                nc.gpsimd.tensor_scalar(out=y_bf16[cell][:], in0=src, scalar1=1.0, scalar2=0.0, op0=MULT, op1=ADD)
-            elif on_scalar:
-                nc.scalar.copy(out=y_bf16[cell][:], in_=src)
-            else:
-                nc.vector.tensor_copy(out=y_bf16[cell][:], in_=src)
-
-        def turn_y(first, count):
-            for pair in range(first, first + count, 2):
-                width = min(2, count)
-                y_bank[pair] = psum.tile([P, width, 2, P], F32, name="bank", tag="bank")
-                for j in range(width):
-                    words = y_bf16[pair + j][:].rearrange("p u q e -> p (u q e)").bitcast(F32)
-                    for u in range(2):
-                        nc.tensor.transpose(y_bank[pair][:, j, u, :], words[:, u * P : (u + 1) * P], ident[:])
-
-        def copy_y(pair, width):
-            y_grouped[pair] = stage.tile([P, width * GROUP], BF16, name="y_grouped", align_bytes=64, bufs=4)
             nc.scalar.copy(
-                out=y_grouped[pair][:].bitcast(F32).rearrange("p (j r u) -> p j r u", j=width, u=2),
-                in_=y_bank[pair][:].rearrange("p j u r -> p j r u"),
+                out=y_grouped[cells][:].bitcast(F32).rearrange("p (j r u) -> p j r u", j=len(cells), u=2),
+                in_=y_banks[cells][:].rearrange("p j u r -> p j r u"),
             )
 
-        def store_words(g, span):
-            dst = out_1[g].rearrange("p m t -> p (m t)").bitcast(I32)
-            nc.sync.dma_start(out=dst[:, span], in_=y_words[g][:, span].bitcast(I32))
-
-        def quantize_y(pair, at, width):
-            g, m = place[pair + at]
-            if m == 0:
-                y_words[g] = keep.tile([P, M], U32, name="y_words%d" % g, align_bytes=64)
+        def quantize_y(cells, source):
+            g, m = place[cells[0]]
+            start, stop = m * P, (m + len(cells)) * P
+            low = max(mark for mark in WORD_MARKS if mark <= start)
+            high = min(mark for mark in WORD_MARKS if mark >= stop)
+            if (g // 2, low) not in y_words:
+                y_words[g // 2, low] = keep.tile(
+                    [P, 2, high - low], U32, name="y_words%d_%d" % (g // 2, low), align_bytes=MX_ALIGN
+                )
+            words = y_words[g // 2, low]
             nc.vector.quantize_mx(
-                out=y_words[g][:, m * P : (m + width) * P].bitcast(FP8X4),
-                scales=y_scales[4 * g :, m * P : (m + width) * P],
-                in_=y_grouped[pair][:, at * GROUP : (at + width) * GROUP],
+                out=words[:, g % 2, start - low : stop - low].bitcast(FP8X4),
+                scales=y_scales[4 * g :, start:stop],
+                in_=source,
             )
-            marks = [0, M // 2, M] if g < GROUPS - 1 else [0, M // 2, M - 2 * P, M]
-            done = (m + width) * P
-            if done in marks:
-                store_words(g, slice(marks[marks.index(done) - 1], done))
-            if g == GROUPS - 1 and done == M:
-                for quad in range(4):
-                    queue = nc.sync if quad < 2 else nc.scalar
-                    queue.dma_start(
-                        out=out_2[:, 4 * quad : 4 * quad + 4, :].bitcast(I32),
-                        in_=y_scales[32 * quad : 32 * quad + 16, :].bitcast(I32),
-                    )
+            if stop == high and g % 2 == 1:
+                dst = out_1.rearrange("g p m t -> p g (m t)").bitcast(I32)
+                nc.sync.dma_start(out=dst[:, g - 1 : g + 1, low:high], in_=words[:].bitcast(I32))
 
-        turn_at, copy_at, quant_at = {}, {}, {}
-        for first, count in sorted(set(turns.values())):
-            when = first + count - 1 + (TURN_LAG if first < TAIL_FROM else TAIL_LAG)
-            turn_at[when] = (first, count)
-            for pair in range(first, first + count, 2):
-                width = min(2, count)
-                copied = when + (pair - first) // 2 * SPREAD
-                copy_at.setdefault(copied, []).append((pair, width))
-                if pair < HALF:
-                    for at in range(2):
-                        quant_at.setdefault(copied + Q_LAG + at, []).append((pair, at, 1))
-                else:
-                    quant_at.setdefault(copied + Q_LAG, []).append((pair, 0, width))
+        def quantize_bank(cells):
+            quantize_y(cells, y_grouped[cells][:])
+
+        early_banks = [
+            (2 * pairs.index((h, m)) + side, 2 * pairs.index((h, m + 1)) + side)
+            for m in range(0, ROW_TILES - 2, 2)
+            for h in range(2)
+            for side in range(2)
+        ]
+        tail_banks = [(cell, cell + 1) for cell in range(CELLS - 8, CELLS - 2, 2)] + [(CELLS - 2,), (CELLS - 1,)]
+
+        def ready(newest_pair):
+            return [cells for cells in early_banks if cells not in y_banks and cells[-1] // 2 <= newest_pair][:2]
 
         bias_lines = load_vector(bias, "bias_lines")
         load_full(0)
@@ -292,79 +287,141 @@ def tile_draft_full_logits_g5_kernel(
         load_head(0)
         load_draft(0)
         load_words(0)
-        load_scales(f_scales_first, slice(0, 2 * GROUP))
+        load_scales(0)
         load_head(1)
         load_full(1)
         load_draft(1)
         load_words(1)
-        load_full(2)
-        load_draft(2)
-        for m in range(3, ROW_TILES):
+        load_head(2)
+        load_head(3)
+        load_scales(1)
+        load_words(2)
+        load_words(3)
+        for m in range(2, PRELOADED):
             load_full(m)
             load_draft(m)
-            if m in (3, 4):
-                load_head(m - 1)
 
-        spread_copy(spread_turn(bias_lines, 0), bias_rows, 0)
+        copy_bias(spread_bias(0), 0)
         for half in range(2):
             turn_x(0, half)
             copy_x(0, half)
-        spread_copy(spread_turn(cap_lines, 0), cap_rows, 0)
-        group_head(0, 0, 1, False)
+        spread_cap(0)
+        group_head(0)
         quantize_x(0, 0, 2)
         quantize_head(0)
         quantize_x(0, 2, 2)
-        group_head(1, 0, 1, False)
+        group_head(1)
 
-        for step in range(max(quant_at) + 1):
-            if step == LATE_AT:
-                load_words(2)
-                load_scales(f_scales_rest, slice(2 * GROUP, V))
-            if step == LATE_AT + 4:
-                load_words(3)
-            ahead = []
-            if step == 1:
-                ahead = [1]
-            elif step >= 2 and step % 2 == 0 and step // 2 + 1 < ROW_TILES:
-                ahead = [step // 2 + 1]
-            if step == 2:
-                quantize_x(1, 0, PASSES)
-            if step == HALF - 2:
-                spread_copy(spread_turn(bias_lines, 1), bias_rows, 1)
-            if step == HALF:
-                spread_copy(spread_turn(cap_lines, 1), cap_rows, 1)
-            for m in ahead:
+        multiply(0)
+        for half in range(2):
+            turn_x(1, half)
+        quantize_head(1)
+        for half in range(2):
+            copy_x(1, half)
+        add_bias(0)
+        squash(0)
+        multiply(1)
+        group_head(2)
+        quantize_x(1, 0, PASSES)
+        bias_bank = spread_bias(1)
+        add_bias(1)
+        quantize_head(2)
+        group_head(3)
+        squash(1)
+        copy_bias(bias_bank, 1)
+        sort_x(SORTED_FROM, 1, nc.scalar.copy)
+        multiply(2)
+        add_bias(2)
+        quantize_head(3)
+        scale_and_store(0, 2)
+        round_y(0, round_on_gpsimd)
+        multiply(3)
+        add_bias(3)
+
+        for step in range(1, STEPS):
+            a, b, c, d = range(4 * step, 4 * step + 4)
+            ahead = step + 1
+            if step + PRELOADED - 1 < ROW_TILES:
+                load_full(step + PRELOADED - 1)
+                load_draft(step + PRELOADED - 1)
+            turned = ready(2 * step - TURN_LAG)
+            if ahead < ROW_TILES:
                 for half in range(2):
-                    turn_x(m, half)
-            if step in turn_at:
-                turn_y(*turn_at[step])
+                    turn_x(ahead, half)
             if step == 1:
-                quantize_head(1)
-            if step < CELLS:
-                multiply(step)
-            if 0 <= step - 1 < CELLS:
-                add_bias(step - 1)
-            if step == 1:
-                squash(0)
-            for m in ahead:
+                spread_cap(1)
+            for cells in turned:
+                turn_y(cells)
+            multiply(a)
+            if ahead < ROW_TILES:
                 for half in range(2):
-                    copy_x(m, half)
-            if 1 <= step - TANH_LAG < CELLS:
-                squash(step - TANH_LAG)
-            if 0 <= step - CAP_LAG < CELLS:
-                scale_and_store(step - CAP_LAG)
-            if step >= 3 and step % 2 == 1 and step // 2 + 1 < ROW_TILES:
-                quantize_x(step // 2 + 1, 0, PASSES)
-            for job in quant_at.get(step, []):
-                quantize_y(*job)
-            cell = step - ROUND_LAG
-            if 0 <= cell < CELLS:
-                round_y(cell, cell % VEC_EVERY != VEC_EVERY - 1 and VEC_HEAD <= cell < CELLS - VEC_TAIL)
-            for job in copy_at.get(step, []):
-                copy_y(*job)
-            g, part = divmod(step - HEAD_AT, 4)
-            if 0 <= g < 2:
-                if part in (0, 2):
-                    group_head(g + 2, part // 2, 2, HS)
-                if part == 3:
-                    quantize_head(g + 2)
+                    copy_x(ahead, half)
+            for cells in turned:
+                copy_y(cells)
+            round_y(a - 3, nc.scalar.copy)
+            squash(a - 2)
+            squash(a - 1)
+            add_bias(a)
+            if ahead < ROW_TILES:
+                quantize_x(ahead, 0, PASSES)
+            for cells in turned[:1]:
+                quantize_bank(cells)
+            squash(a)
+            multiply(b)
+            add_bias(b)
+            for cells in turned[1:]:
+                quantize_bank(cells)
+            if ahead + 1 < ROW_TILES:
+                sort_x(ahead + 1, 0, nc.vector.tensor_copy)
+            squash(b)
+            scale_and_store(a - 2, 2)
+            round_y(a - 2, round_on_gpsimd)
+            if ahead + 2 < ROW_TILES:
+                sort_x(ahead + 2, 1, nc.scalar.copy)
+            round_y(a - 1, nc.scalar.copy)
+            if step < STEPS - 1:
+                multiply(c)
+                add_bias(c)
+                scale_and_store(a, 2)
+                round_y(a, round_on_gpsimd)
+                multiply(d)
+                add_bias(d)
+
+        turned = ready(2 * STEPS - TURN_LAG)
+        for cells in turned:
+            turn_y(cells)
+        multiply(c)
+        add_bias(c)
+        multiply(d)
+        scale_and_store(a, 1)
+        round_y(a, round_on_gpsimd)
+        copy_y(turned[0])
+        squash(c)
+        add_bias(d)
+        copy_y(turned[1])
+        squash(d)
+        turn_y(tail_banks[0])
+        turn_y(tail_banks[1])
+        scale_and_store(b, 1)
+        quantize_bank(turned[0])
+        round_y(b, nc.scalar.copy)
+        scale_and_store(c, 1)
+        quantize_bank(turned[1])
+        round_y(c, round_on_gpsimd)
+        scale_and_store(d, 1)
+        turn_y(tail_banks[2])
+        round_y(d, nc.vector.tensor_copy)
+        turn_y(tail_banks[3])
+        turn_y(tail_banks[4])
+        for cells in sorted(tail_banks, key=lambda cells: place[cells[0]]):
+            copy_y(cells)
+        last_cells = [(place[cell], cells, j) for cells in tail_banks for j, cell in enumerate(cells)]
+        for where, cells, j in sorted(last_cells):
+            quantize_y(cells[j : j + 1], y_grouped[cells][:, cols(j)])
+
+        for quad in range(QUADRANTS):
+            queue = nc.sync if quad < QUADRANTS // 2 else nc.scalar
+            queue.dma_start(
+                out=out_2[:, 4 * quad : 4 * quad + 4, :].bitcast(I32),
+                in_=y_scales[32 * quad : 32 * quad + 16, :].bitcast(I32),
+            )

@@ -30,8 +30,9 @@ BANKS = 8
 QUADRANTS = 4
 MX_ALIGN = 64
 
-PRELOADED = 5
-SORTED_FROM = 3
+LEADING = 3
+PRELOADED = 4
+SCALE_PARTS = [(0, 1), (1, 2), (2, 4)]
 TURN_LAG = 4
 WORD_MARKS = [0, M // 2, M - 2 * P, M]
 
@@ -51,19 +52,22 @@ def tile_draft_full_logits_g5_kernel(
         make_identity(nc, ident[:])
 
         f_scales = []
-        for h in range(2):
-            plane = keep.tile([P, FULL_PASSES, WIDE], U8, name="f_scales%d" % h, align_bytes=MX_ALIGN)
+        for first, stop in SCALE_PARTS:
+            plane = keep.tile(
+                [P, FULL_PASSES, (stop - first) * GROUP], U8, name="f_scales%d" % first, align_bytes=MX_ALIGN
+            )
             nc.vector.memset(plane[:].rearrange("p c n -> p (c n)").bitcast(I32), 0)
             f_scales.append(plane)
         bias_rows = keep.tile([P, V], BF16, name="bias_rows")
         y_scales = keep.tile([P, M], U8, name="y_scales", align_bytes=MX_ALIGN)
 
-        x_raw, x_sorted, x_banks, x_grouped, x_codes, x_scales = {}, {}, {}, {}, {}, {}
+        x_raw, x_banks, x_grouped, x_codes, x_scales = {}, {}, {}, {}, {}
         f_words, h_raw, h_grouped, h_codes, h_scales = {}, {}, {}, {}, {}
         cap_banks, acc, logits, squashed, y_f32 = {}, {}, {}, {}, {}
         y_bf16, y_banks, y_grouped, y_words = {}, {}, {}, {}
 
-        pairs = [(0, 0), (0, 1), (1, 0), (1, 1)] + [(h, m) for m in range(2, ROW_TILES) for h in range(2)]
+        pairs = [(h, m) for h in range(2) for m in range(LEADING)]
+        pairs.extend((h, m) for m in range(LEADING, ROW_TILES) for h in range(2))
         place = [(2 * h + side, m) for h, m in pairs for side in range(2)]
 
         free_banks = list(range(BANKS))
@@ -97,11 +101,12 @@ def tile_draft_full_logits_g5_kernel(
             src = full_words.rearrange("c p n -> p c n")[:, :, 2 * g * GROUP : 2 * (g + 1) * GROUP]
             nc.sync.dma_start(out=f_words[g][:].bitcast(I32), in_=src.bitcast(I32))
 
-        def load_scales(h):
-            rows = full_scales.rearrange("c q n -> q c n")[:, :, wide(h)]
+        def load_scales(part):
+            first, stop = SCALE_PARTS[part]
+            rows = full_scales.rearrange("c q n -> q c n")[:, :, first * GROUP : stop * GROUP]
             for quad in range(QUADRANTS):
                 nc.sync.dma_start(
-                    out=f_scales[h][32 * quad : 32 * quad + 4, :, :].bitcast(I32),
+                    out=f_scales[part][32 * quad : 32 * quad + 4, :, :].bitcast(I32),
                     in_=rows[4 * quad : 4 * quad + 4, :, :].bitcast(I32),
                 )
 
@@ -129,20 +134,12 @@ def tile_draft_full_logits_g5_kernel(
                 nc.tensor.transpose(cap_banks[h][:, :, i], words[:, i : i + 1].to_broadcast([P, P]), ident[:])
 
 
-        def x_words(m, half):
-            words = x_raw[m][:, wide(half)].bitcast(F32)
-            return words.rearrange("p (c q u) -> p c u q", c=2, u=2)
-
-        def sort_x(m, half, copy):
-            x_sorted[m, half] = stage.tile([P, 2, 2, P], F32, name="x_sorted", bufs=6)
-            copy(out=x_sorted[m, half][:], in_=x_words(m, half))
-
         def turn_x(m, half):
             x_banks[m, half] = next_bank([P, 2, 2, P])
-            source = x_sorted[m, half][:] if m >= SORTED_FROM else x_words(m, half)
+            words = x_raw[m][:, wide(half)].bitcast(F32).rearrange("p (c q u) -> p c u q", c=2, u=2)
             for c in range(2):
                 for u in range(2):
-                    nc.tensor.transpose(x_banks[m, half][:, c, u, :], source[:, c, u, :], ident[:])
+                    nc.tensor.transpose(x_banks[m, half][:, c, u, :], words[:, c, u, :], ident[:])
 
         def copy_x(m, half):
             if half == 0:
@@ -164,9 +161,9 @@ def tile_draft_full_logits_g5_kernel(
             )
 
 
-        def group_head(g):
+        def group_head(g, copy):
             h_grouped[g] = stage.tile([P, GROUP, PACK], BF16, name="h_grouped", align_bytes=MX_ALIGN, bufs=2)
-            nc.vector.tensor_copy(
+            copy(
                 out=h_grouped[g][:].rearrange("p (a i) t -> p a t i", i=4),
                 in_=h_raw[g][:].rearrange("p t (a i) -> p a t i", i=4),
             )
@@ -184,9 +181,11 @@ def tile_draft_full_logits_g5_kernel(
         def multiply(cell):
             g, m = place[cell]
             acc[cell] = next_bank([P, GROUP])
+            part = max(i for i, (first, stop) in enumerate(SCALE_PARTS) if first <= g)
             for c in range(PASSES):
                 if c < FULL_PASSES:
-                    rhs, rhs_scale = f_words[g][:, c, :].bitcast(FP4X4), f_scales[g // 2][:, c, cols(g % 2)]
+                    rhs = f_words[g][:, c, :].bitcast(FP4X4)
+                    rhs_scale = f_scales[part][:, c, cols(g - SCALE_PARTS[part][0])]
                 else:
                     rhs, rhs_scale = h_codes[g][:].bitcast(FP8X4), h_scales[g][:]
                 nc.tensor.matmul_mx(
@@ -270,12 +269,15 @@ def tile_draft_full_logits_g5_kernel(
         def quantize_bank(cells):
             quantize_y(cells, y_grouped[cells][:])
 
-        early_banks = [
-            (2 * pairs.index((h, m)) + side, 2 * pairs.index((h, m + 1)) + side)
-            for m in range(0, ROW_TILES - 2, 2)
-            for h in range(2)
-            for side in range(2)
-        ]
+        early_banks = sorted(
+            (
+                (2 * pairs.index((h, m)) + side, 2 * pairs.index((h, m + 1)) + side)
+                for m in range(0, ROW_TILES - 2, 2)
+                for h in range(2)
+                for side in range(2)
+            ),
+            key=lambda cells: cells[-1],
+        )
         tail_banks = [(cell, cell + 1) for cell in range(CELLS - 8, CELLS - 2, 2)] + [(CELLS - 2,), (CELLS - 1,)]
 
         def ready(newest_pair):
@@ -291,26 +293,28 @@ def tile_draft_full_logits_g5_kernel(
         load_head(1)
         load_full(1)
         load_draft(1)
+        load_scales(1)
         load_words(1)
+        load_full(2)
+        load_draft(2)
         load_head(2)
         load_head(3)
-        load_scales(1)
+        load_scales(2)
         load_words(2)
         load_words(3)
-        for m in range(2, PRELOADED):
-            load_full(m)
-            load_draft(m)
+        load_full(3)
+        load_draft(3)
 
         copy_bias(spread_bias(0), 0)
         for half in range(2):
             turn_x(0, half)
             copy_x(0, half)
         spread_cap(0)
-        group_head(0)
+        group_head(0, nc.vector.tensor_copy)
         quantize_x(0, 0, 2)
         quantize_head(0)
         quantize_x(0, 2, 2)
-        group_head(1)
+        group_head(1, nc.vector.tensor_copy)
 
         multiply(0)
         for half in range(2):
@@ -321,18 +325,17 @@ def tile_draft_full_logits_g5_kernel(
         add_bias(0)
         squash(0)
         multiply(1)
-        group_head(2)
         quantize_x(1, 0, PASSES)
-        bias_bank = spread_bias(1)
+        for half in range(2):
+            turn_x(2, half)
+            copy_x(2, half)
         add_bias(1)
-        quantize_head(2)
-        group_head(3)
         squash(1)
-        copy_bias(bias_bank, 1)
-        sort_x(SORTED_FROM, 1, nc.scalar.copy)
         multiply(2)
+        group_head(2, nc.vector.tensor_copy)
+        quantize_x(2, 0, PASSES)
         add_bias(2)
-        quantize_head(3)
+        quantize_head(2)
         scale_and_store(0, 2)
         round_y(0, round_on_gpsimd)
         multiply(3)
@@ -341,43 +344,46 @@ def tile_draft_full_logits_g5_kernel(
         for step in range(1, STEPS):
             a, b, c, d = range(4 * step, 4 * step + 4)
             ahead = step + 1
+            new_rows = LEADING <= ahead < ROW_TILES
             if step + PRELOADED - 1 < ROW_TILES:
                 load_full(step + PRELOADED - 1)
                 load_draft(step + PRELOADED - 1)
             turned = ready(2 * step - TURN_LAG)
-            if ahead < ROW_TILES:
+            if new_rows:
                 for half in range(2):
                     turn_x(ahead, half)
             if step == 1:
+                bias_bank = spread_bias(1)
                 spread_cap(1)
             for cells in turned:
                 turn_y(cells)
             multiply(a)
-            if ahead < ROW_TILES:
+            if new_rows:
                 for half in range(2):
                     copy_x(ahead, half)
             for cells in turned:
                 copy_y(cells)
+            if step == 1:
+                group_head(3, nc.scalar.copy)
+                copy_bias(bias_bank, 1)
             round_y(a - 3, nc.scalar.copy)
             squash(a - 2)
             squash(a - 1)
             add_bias(a)
-            if ahead < ROW_TILES:
+            if new_rows:
                 quantize_x(ahead, 0, PASSES)
             for cells in turned[:1]:
                 quantize_bank(cells)
             squash(a)
             multiply(b)
             add_bias(b)
+            if step == 1:
+                quantize_head(3)
             for cells in turned[1:]:
                 quantize_bank(cells)
-            if ahead + 1 < ROW_TILES:
-                sort_x(ahead + 1, 0, nc.vector.tensor_copy)
             squash(b)
             scale_and_store(a - 2, 2)
             round_y(a - 2, round_on_gpsimd)
-            if ahead + 2 < ROW_TILES:
-                sort_x(ahead + 2, 1, nc.scalar.copy)
             round_y(a - 1, nc.scalar.copy)
             if step < STEPS - 1:
                 multiply(c)

from contextlib import ExitStack

import concourse.mybir as mybir
from concourse.masks import make_identity

M, K, R, V = 1024, 1536, 512, 2048
FLOPS = 2 * M * (K + R) * V

F32 = mybir.dt.float32
BF16 = mybir.dt.bfloat16
I32 = mybir.dt.int32
U32 = mybir.dt.uint32
U8 = mybir.dt.uint8
FP8X4 = mybir.dt.float8_e4m3fn_x4
FP4X4 = mybir.dt.float4_e2m1fn_x4
ADD = mybir.AluOpType.add
MULT = mybir.AluOpType.mult
TANH = mybir.ActivationFunctionType.Tanh

P = 128
PACK = 4
GROUP = P * PACK
WIDE = 2 * GROUP
FULL_PASSES = K // GROUP
PASSES = FULL_PASSES + R // GROUP
ROW_TILES = M // P
CELLS = ROW_TILES * V // GROUP
STEPS = CELLS // 4
BANKS = 8
QUADRANTS = 4
MX_ALIGN = 64

LEADING = 3
PRELOADED = 4
SCALE_PARTS = [(0, 1), (1, 2), (2, 4)]
TURN_LAG = 4
WORD_MARKS = [0, M // 2, M - 2 * P, M]


def tile_draft_full_logits_g5_kernel(
    tc, draft_state, draft_head, full_state, full_words, full_scales, bias, cap, out_0, out_1, out_2
):
    nc = tc.nc

    with ExitStack() as ctx:
        keep = ctx.enter_context(tc.tile_pool(name="keep", bufs=1))
        stage = ctx.enter_context(tc.tile_pool(name="stage", bufs=3))
        psum = ctx.enter_context(tc.psum_pool(name="psum", bufs=1))
        ctx.enter_context(tc.manual_schedule())

        ident = keep.tile([P, P], F32, name="ident")
        make_identity(nc, ident[:])

        f_scales = []
        for first, stop in SCALE_PARTS:
            plane = keep.tile(
                [P, FULL_PASSES, (stop - first) * GROUP], U8, name="f_scales%d" % first, align_bytes=MX_ALIGN
            )
            nc.vector.memset(plane[:].rearrange("p c n -> p (c n)").bitcast(I32), 0)
            f_scales.append(plane)
        bias_rows = keep.tile([P, V], BF16, name="bias_rows")
        y_scales = keep.tile([P, M], U8, name="y_scales", align_bytes=MX_ALIGN)

        x_raw, x_banks, x_grouped, x_codes, x_scales = {}, {}, {}, {}, {}
        f_words, h_raw, h_grouped, h_codes, h_scales = {}, {}, {}, {}, {}
        cap_banks, acc, logits, squashed, y_f32 = {}, {}, {}, {}, {}
        y_bf16, y_banks, y_grouped, y_words = {}, {}, {}, {}

        pairs = [(h, m) for h in range(2) for m in range(LEADING)]
        pairs.extend((h, m) for m in range(LEADING, ROW_TILES) for h in range(2))
        place = [(2 * h + side, m) for h, m in pairs for side in range(2)]

        free_banks = list(range(BANKS))

        def next_bank(shape, hold=False):
            number = free_banks.pop(0)
            if not hold:
                free_banks.append(number)
            return psum.tile(shape, F32, name="bank%d" % number)

        def cols(g):
            return slice(g * GROUP, (g + 1) * GROUP)

        def wide(h):
            return slice(h * WIDE, (h + 1) * WIDE)


        def load_full(m):
            x_raw[m] = keep.tile([P, K + R], BF16, name="x_raw%d" % m)
            nc.sync.dma_start(out=x_raw[m][:, :K], in_=full_state[m * P : (m + 1) * P, :])

        def load_draft(m):
            nc.sync.dma_start(out=x_raw[m][:, K:], in_=draft_state[m * P : (m + 1) * P, :])

        def load_head(g):
            h_raw[g] = keep.tile([P, PACK, GROUP], BF16, name="h_raw%d" % g)
            nc.sync.dma_start(out=h_raw[g][:], in_=draft_head[:, cols(g)].rearrange("(p t) v -> p t v", t=PACK))

        def load_words(g):
            f_words[g] = keep.tile([P, FULL_PASSES, 2 * GROUP], U8, name="f_words%d" % g, align_bytes=MX_ALIGN)
            src = full_words.rearrange("c p n -> p c n")[:, :, 2 * g * GROUP : 2 * (g + 1) * GROUP]
            nc.sync.dma_start(out=f_words[g][:].bitcast(I32), in_=src.bitcast(I32))

        def load_scales(part):
            first, stop = SCALE_PARTS[part]
            rows = full_scales.rearrange("c q n -> q c n")[:, :, first * GROUP : stop * GROUP]
            for quad in range(QUADRANTS):
                nc.sync.dma_start(
                    out=f_scales[part][32 * quad : 32 * quad + 4, :, :].bitcast(I32),
                    in_=rows[4 * quad : 4 * quad + 4, :, :].bitcast(I32),
                )

        def load_vector(vector, name):
            lines = keep.tile([P, 2, 2 * PACK], BF16, name=name)
            nc.sync.dma_start(out=lines[:], in_=vector.rearrange("(h n e) -> n h e", h=2, n=P))
            return lines


        def spread_bias(h):
            bank = next_bank([P, PACK, P])
            words = bias_lines[:, h, :].bitcast(F32)
            for i in range(PACK):
                nc.tensor.transpose(bank[:, i, :], words[:, i : i + 1].to_broadcast([P, P]), ident[:])
            return bank

        def copy_bias(bank, h):
            words = bias_rows[:, wide(h)].bitcast(F32).rearrange("p (n i) -> p n i", i=PACK)
            nc.scalar.copy(out=words, in_=bank[:].rearrange("p i n -> p n i"))

        def spread_cap(h):
            cap_banks[h] = next_bank([P, P, PACK], hold=True)
            words = cap_lines[:, h, :].bitcast(F32)
            for i in range(PACK):
                nc.tensor.transpose(cap_banks[h][:, :, i], words[:, i : i + 1].to_broadcast([P, P]), ident[:])


        def turn_x(m, half):
            x_banks[m, half] = next_bank([P, 2, 2, P])
            words = x_raw[m][:, wide(half)].bitcast(F32).rearrange("p (c q u) -> p c u q", c=2, u=2)
            for c in range(2):
                for u in range(2):
                    nc.tensor.transpose(x_banks[m, half][:, c, u, :], words[:, c, u, :], ident[:])

        def copy_x(m, half):
            if half == 0:
                x_grouped[m] = stage.tile([P, PASSES * GROUP], BF16, name="x_grouped", align_bytes=MX_ALIGN)
            nc.scalar.copy(
                out=x_grouped[m][:, wide(half)].bitcast(F32).rearrange("p (c r u) -> p c r u", c=2, u=2),
                in_=x_banks[m, half][:].rearrange("p c u r -> p c r u"),
            )

        def quantize_x(m, first_pass, passes):
            if first_pass == 0:
                x_codes[m] = keep.tile([P, PASSES * P], U32, name="x_codes%d" % m, align_bytes=MX_ALIGN)
                x_scales[m] = keep.tile([P, PASSES * P], U8, name="x_scales%d" % m, align_bytes=MX_ALIGN)
            span = slice(first_pass * P, (first_pass + passes) * P)
            nc.vector.quantize_mx(
                out=x_codes[m][:, span].bitcast(FP8X4),
                scales=x_scales[m][:, span],
                in_=x_grouped[m][:, first_pass * GROUP : (first_pass + passes) * GROUP],
            )


        def group_head(g, copy):
            h_grouped[g] = stage.tile([P, GROUP, PACK], BF16, name="h_grouped", align_bytes=MX_ALIGN, bufs=2)
            copy(
                out=h_grouped[g][:].rearrange("p (a i) t -> p a t i", i=4),
                in_=h_raw[g][:].rearrange("p t (a i) -> p a t i", i=4),
            )

        def quantize_head(g):
            h_codes[g] = keep.tile([P, GROUP], U32, name="h_codes%d" % g, align_bytes=MX_ALIGN)
            h_scales[g] = keep.tile([P, GROUP], U8, name="h_scales%d" % g, align_bytes=MX_ALIGN)
            nc.vector.quantize_mx(
                out=h_codes[g][:].bitcast(FP8X4),
                scales=h_scales[g][:],
                in_=h_grouped[g][:].rearrange("p v t -> p (v t)"),
            )


        def multiply(cell):
            g, m = place[cell]
            acc[cell] = next_bank([P, GROUP])
            part = max(i for i, (first, stop) in enumerate(SCALE_PARTS) if first <= g)
            for c in range(PASSES):
                if c < FULL_PASSES:
                    rhs = f_words[g][:, c, :].bitcast(FP4X4)
                    rhs_scale = f_scales[part][:, c, cols(g - SCALE_PARTS[part][0])]
                else:
                    rhs, rhs_scale = h_codes[g][:].bitcast(FP8X4), h_scales[g][:]
                nc.tensor.matmul_mx(
                    out=acc[cell][:],
                    lhsT=x_codes[m][:, c * P : (c + 1) * P].bitcast(FP8X4),
                    lhsT_scale=x_scales[m][:, c * P : (c + 1) * P],
                    rhs=rhs,
                    rhs_scale=rhs_scale,
                    start=(c == 0),
                    stop=(c == PASSES - 1),
                )

        def add_bias(cell):
            pair, side = divmod(cell, 2)
            if side == 0:
                logits[pair] = stage.tile([P, WIDE], F32, name="logits")
            nc.vector.tensor_tensor(
                out=logits[pair][:, cols(side)], in0=acc[cell][:], in1=bias_rows[:, cols(place[cell][0])], op=ADD
            )

        def squash(cell):
            pair, side = divmod(cell, 2)
            if side == 0:
                squashed[pair] = stage.tile([P, WIDE], F32, name="squashed")
            nc.scalar.activation(out=squashed[pair][:, cols(side)], in_=logits[pair][:, cols(side)], func=TANH)

        def scale_and_store(cell, count):
            pair, side = divmod(cell, 2)
            h, m = pairs[pair]
            if side == 0:
                y_f32[pair] = stage.tile([P, WIDE], F32, name="y_f32", bufs=5)
            span = slice(side * GROUP, (side + count) * GROUP)
            caps = cap_banks[h][:].rearrange("p n i -> p (n i)").bitcast(BF16)
            nc.vector.tensor_tensor(out=y_f32[pair][:, span], in0=squashed[pair][:, span], in1=caps[:, span], op=MULT)
            nc.sync.dma_start(out=out_0[m * P : (m + 1) * P, wide(h)][:, span], in_=y_f32[pair][:, span])


        def round_on_gpsimd(out, in_):
            nc.gpsimd.tensor_scalar(out=out, in0=in_, scalar1=1.0, scalar2=-0.0, op0=MULT, op1=ADD)

        def round_y(cell, convert):
            y_bf16[cell] = stage.tile([P, 2, P, 2], BF16, name="y_bf16", bufs=14)
            src = y_f32[cell // 2][:, cols(cell % 2)].rearrange("p (q u e) -> p u q e", u=2, e=2)
            convert(out=y_bf16[cell][:], in_=src)

        def turn_y(cells):
            y_banks[cells] = next_bank([P, len(cells), 2, P])
            for j, cell in enumerate(cells):
                words = y_bf16[cell][:].rearrange("p u q e -> p u (q e)").bitcast(F32)
                for u in range(2):
                    nc.tensor.transpose(y_banks[cells][:, j, u, :], words[:, u, :], ident[:])

        def copy_y(cells):
            y_grouped[cells] = stage.tile(
                [P, len(cells) * GROUP], BF16, name="y_grouped", align_bytes=MX_ALIGN, bufs=6
            )
            nc.scalar.copy(
                out=y_grouped[cells][:].bitcast(F32).rearrange("p (j r u) -> p j r u", j=len(cells), u=2),
                in_=y_banks[cells][:].rearrange("p j u r -> p j r u"),
            )

        def quantize_y(cells, source):
            g, m = place[cells[0]]
            start, stop = m * P, (m + len(cells)) * P
            low = max(mark for mark in WORD_MARKS if mark <= start)
            high = min(mark for mark in WORD_MARKS if mark >= stop)
            if (g // 2, low) not in y_words:
                y_words[g // 2, low] = keep.tile(
                    [P, 2, high - low], U32, name="y_words%d_%d" % (g // 2, low), align_bytes=MX_ALIGN
                )
            words = y_words[g // 2, low]
            nc.vector.quantize_mx(
                out=words[:, g % 2, start - low : stop - low].bitcast(FP8X4),
                scales=y_scales[4 * g :, start:stop],
                in_=source,
            )
            if stop == high and g % 2 == 1:
                dst = out_1.rearrange("g p m t -> p g (m t)").bitcast(I32)
                nc.sync.dma_start(out=dst[:, g - 1 : g + 1, low:high], in_=words[:].bitcast(I32))

        def quantize_bank(cells):
            quantize_y(cells, y_grouped[cells][:])

        early_banks = sorted(
            (
                (2 * pairs.index((h, m)) + side, 2 * pairs.index((h, m + 1)) + side)
                for m in range(0, ROW_TILES - 2, 2)
                for h in range(2)
                for side in range(2)
            ),
            key=lambda cells: cells[-1],
        )
        tail_banks = [(cell, cell + 1) for cell in range(CELLS - 8, CELLS - 2, 2)] + [(CELLS - 2,), (CELLS - 1,)]

        def ready(newest_pair):
            return [cells for cells in early_banks if cells not in y_banks and cells[-1] // 2 <= newest_pair][:2]

        bias_lines = load_vector(bias, "bias_lines")
        load_full(0)
        cap_lines = load_vector(cap, "cap_lines")
        load_head(0)
        load_draft(0)
        load_words(0)
        load_scales(0)
        load_head(1)
        load_full(1)
        load_draft(1)
        load_scales(1)
        load_words(1)
        load_full(2)
        load_draft(2)
        load_head(2)
        load_head(3)
        load_scales(2)
        load_words(2)
        load_words(3)
        load_full(3)
        load_draft(3)

        copy_bias(spread_bias(0), 0)
        for half in range(2):
            turn_x(0, half)
            copy_x(0, half)
        spread_cap(0)
        group_head(0, nc.vector.tensor_copy)
        quantize_x(0, 0, 2)
        quantize_head(0)
        quantize_x(0, 2, 2)
        group_head(1, nc.vector.tensor_copy)

        multiply(0)
        for half in range(2):
            turn_x(1, half)
        quantize_head(1)
        for half in range(2):
            copy_x(1, half)
        add_bias(0)
        squash(0)
        multiply(1)
        quantize_x(1, 0, PASSES)
        for half in range(2):
            turn_x(2, half)
            copy_x(2, half)
        add_bias(1)
        squash(1)
        multiply(2)
        group_head(2, nc.vector.tensor_copy)
        quantize_x(2, 0, PASSES)
        add_bias(2)
        quantize_head(2)
        scale_and_store(0, 2)
        round_y(0, round_on_gpsimd)
        multiply(3)
        add_bias(3)

        for step in range(1, STEPS):
            a, b, c, d = range(4 * step, 4 * step + 4)
            ahead = step + 1
            new_rows = LEADING <= ahead < ROW_TILES
            if step + PRELOADED - 1 < ROW_TILES:
                load_full(step + PRELOADED - 1)
                load_draft(step + PRELOADED - 1)
            turned = ready(2 * step - TURN_LAG)
            if new_rows:
                for half in range(2):
                    turn_x(ahead, half)
            if step == 1:
                bias_bank = spread_bias(1)
                spread_cap(1)
            for cells in turned:
                turn_y(cells)
            multiply(a)
            if new_rows:
                for half in range(2):
                    copy_x(ahead, half)
            for cells in turned:
                copy_y(cells)
            if step == 1:
                group_head(3, nc.scalar.copy)
                copy_bias(bias_bank, 1)
            round_y(a - 3, nc.scalar.copy)
            squash(a - 2)
            squash(a - 1)
            add_bias(a)
            if new_rows:
                quantize_x(ahead, 0, PASSES)
            for cells in turned[:1]:
                quantize_bank(cells)
            squash(a)
            multiply(b)
            add_bias(b)
            if step == 1:
                quantize_head(3)
            for cells in turned[1:]:
                quantize_bank(cells)
            squash(b)
            scale_and_store(a - 2, 2)
            round_y(a - 2, round_on_gpsimd)
            round_y(a - 1, nc.scalar.copy)
            if step < STEPS - 1:
                multiply(c)
                add_bias(c)
                scale_and_store(a, 2)
                round_y(a, round_on_gpsimd)
                multiply(d)
                add_bias(d)

        turned = ready(2 * STEPS - TURN_LAG)
        for cells in turned:
            turn_y(cells)
        multiply(c)
        add_bias(c)
        multiply(d)
        scale_and_store(a, 1)
        round_y(a, round_on_gpsimd)
        copy_y(turned[0])
        squash(c)
        add_bias(d)
        copy_y(turned[1])
        squash(d)
        turn_y(tail_banks[0])
        turn_y(tail_banks[1])
        scale_and_store(b, 1)
        quantize_bank(turned[0])
        round_y(b, nc.scalar.copy)
        scale_and_store(c, 1)
        quantize_bank(turned[1])
        round_y(c, round_on_gpsimd)
        scale_and_store(d, 1)
        turn_y(tail_banks[2])
        round_y(d, nc.vector.tensor_copy)
        turn_y(tail_banks[3])
        turn_y(tail_banks[4])
        for cells in sorted(tail_banks, key=lambda cells: place[cells[0]]):
            copy_y(cells)
        last_cells = [(place[cell], cells, j) for cells in tail_banks for j, cell in enumerate(cells)]
        for where, cells, j in sorted(last_cells):
            quantize_y(cells[j : j + 1], y_grouped[cells][:, cols(j)])

        for quad in range(QUADRANTS):
            queue = nc.sync if quad < QUADRANTS // 2 else nc.scalar
            queue.dma_start(
                out=out_2[:, 4 * quad : 4 * quad + 4, :].bitcast(I32),
                in_=y_scales[32 * quad : 32 * quad + 16, :].bitcast(I32),
            )
